import numpy as np
import ml_dtypes


def mxq(x, axis, fmt="e4m3"):
    dtype, down = {"e4m3": (ml_dtypes.float8_e4m3fn, 7), "e5m2": (ml_dtypes.float8_e5m2, 14)}[fmt]
    v = np.moveaxis(np.asarray(x, np.float32).astype(ml_dtypes.bfloat16).astype(np.float64), axis, -1)
    blocks = v.reshape(v.shape[:-1] + (-1, 32))
    amax = np.abs(blocks).max(-1, keepdims=True)
    byte = np.maximum(np.where(amax > 0, np.frexp(amax)[1] - 1 + 127, 0) - down, 1)
    scale = np.exp2(byte - 127.0)
    codes = (blocks / scale).astype(np.float32).astype(dtype).astype(np.float64)
    return np.moveaxis((codes * scale).reshape(v.shape), -1, axis)


WIDE = False


def mx_kscale(k):
    if not WIDE:
        return np.ones(k)
    levels = np.array([10, -10, 5, -5, 0])
    if k % 512:
        return np.exp2(np.random.permutation(np.resize(levels, k // 32))).repeat(32)
    a = np.empty((k // 512, 16))
    for p in range(k // 512):
        a[p, :8] = np.random.permutation(np.resize(levels, 8))
        for g in range(8):
            far = levels[np.abs(levels - a[p, g]) >= 10]
            a[p, g + 8] = far[np.random.randint(len(far))]
    return np.exp2(a.ravel()).repeat(32)


def f64(x):
    return np.asarray(x).astype(np.float64)


def striped(idx):
    return np.tile(idx.reshape(-1, 16).T, (8, 1)).astype(np.uint16)


def unstriped(offs):
    return offs[:16].T.reshape(-1).astype(np.int64)


E2M1 = np.array([0.0, 0.5, 1.0, 1.5, 2.0, 3.0, 4.0, 6.0, -0.0, -0.5, -1.0, -1.5, -2.0, -3.0, -4.0, -6.0])


def pack_weight(w, fmt):
    k, n = w.shape
    w = f64(np.asarray(w, np.float32).astype(ml_dtypes.bfloat16)).reshape(k // 32, 32, n)
    amax = np.abs(w).max(1)
    if fmt == "e4m3":
        byte = np.frexp(amax)[1] - 1 + 127 - 7
    else:
        mant, ex = np.frexp(amax / 6.0)
        byte = np.where(mant > 0.5, ex, ex - 1) + 127
    byte = np.clip(np.where(amax > 0, byte, 1), 1, 254)
    scaled = (w * np.exp2(127.0 - byte)[:, None, :]).reshape(k, n).astype(np.float32)
    by_word = np.ascontiguousarray(scaled.reshape(k // 512, 128, 4, n).transpose(0, 1, 3, 2))
    if fmt == "e4m3":
        words = by_word.astype(ml_dtypes.float8_e4m3fn).view(np.uint8)
    else:
        c = by_word.astype(ml_dtypes.float4_e2m1fn).view(np.uint8) & 0xF
        words = (c[..., 0::2] | (c[..., 1::2] << 4)).reshape(k // 512, 128, 2 * n)
    return np.ascontiguousarray(words), np.ascontiguousarray(byte.astype(np.uint8).reshape(k // 512, 16, n))


def unpack_weight(words, scales, fmt):
    g, _, n = scales.shape
    words = np.ascontiguousarray(words).reshape(g, 128, n, -1)
    if fmt == "e4m3":
        vals = words.view(ml_dtypes.float8_e4m3fn).astype(np.float64)
    else:
        nib = np.empty((g, 128, n, 4), np.uint8)
        nib[..., 0::2] = words & 0xF
        nib[..., 1::2] = words >> 4
        vals = E2M1[nib]
    vals = vals * np.repeat(np.exp2(scales.astype(np.float64) - 127.0), 8, axis=1)[..., None]
    return vals.transpose(0, 1, 3, 2).reshape(g * 512, n)


def gelu(v):
    return 0.5 * v * (1.0 + np.tanh(np.sqrt(2.0 / np.pi) * (v + 0.044715 * v**3)))


T, S, S2, K = 4096, 512, 1024, 1024


def setup_inputs():
    n = np.random.standard_normal
    s = mx_kscale(K)[:, None]
    d = {}
    d["tab_words"], d["tab_scales"] = pack_weight(n((K, T)) * s, "e4m3")
    d["offs"] = striped(np.random.permutation(T)[:S])
    d["offs2"] = striped(np.random.permutation(T)[:S2])
    d["w1"] = (n((K, K)) / s / s.T / K).astype(np.float32)
    d["w4_words"], d["w4_scales"] = pack_weight(n((K, K)) / s / K, "e2m1")
    d["gn"] = (np.exp(0.3 * n(K)) / s[:, 0]).astype(np.float32)
    d["w3"] = (1.8 * n((K, S2)) / s / K ** 0.5).astype(np.float32)
    d["b3"] = (0.8 * n(S2)).astype(np.float32)
    return d


def reference(tab_words, tab_scales, offs, offs2, w1, w4_words, w4_scales, gn, w3, b3):
    tw = unpack_weight(tab_words, tab_scales, "e4m3")
    v = tw[:, unstriped(offs)]
    v2 = tw[:, unstriped(offs2)]
    w4 = unpack_weight(w4_words, w4_scales, "e2m1")
    asked = mxq(f64(w1), 0, "e4m3").T @ v
    own = w4.T @ v
    h = np.maximum(asked, f64(gn)[:, None] * own)
    e = v2.T @ mxq(h, 0, "e4m3")
    lean = (mxq(f64(w3), 0, "e4m3").T @ v) + f64(b3)[:, None]
    return e * (1.0 / (1.0 + np.exp(-lean)))

@@ -1,0 +1,294 @@
+from contextlib import ExitStack
+
+import concourse.mybir as mybir
+from concourse.masks import make_identity
+
+K, T, S, S2 = 1024, 4096, 512, 1024
+FLOPS = 2 * K * S * (K + K + S2 + S2)
+
+F32 = mybir.dt.float32
+BF16 = mybir.dt.bfloat16
+I32 = mybir.dt.int32
+U32 = mybir.dt.uint32
+U16 = mybir.dt.uint16
+U8 = mybir.dt.uint8
+FP8X4 = mybir.dt.float8_e4m3fn_x4
+FP4X4 = mybir.dt.float4_e2m1fn_x4
+ACT = mybir.ActivationFunctionType
+ALU = mybir.AluOpType
+
+P = 128
+PACK = 4
+KP = P * PACK
+PASSES = K // KP
+W3_WIDTHS = (512, 256, 256)
+SLOT = 4096
+W1_SLOTS = {(0, 0): 8, (0, 1): 8, (1, 0): 0, (1, 1): 2}
+W3_SLOTS = {(0, 0): 10, (0, 1): 4, (1, 0): 6, (1, 1): 7, (2, 0): 8, (2, 1): 0}
+V_COL, V2_COL, W4_COL = 0, S, S + S2
+PLANE = S + S2 + K
+
+
+def tile_list_roommate_fit_scores_kernel(
+    tc, tab_words, tab_scales, offs, offs2, w1, w4_words, w4_scales, gn, w3, b3, out
+):
+    nc = tc.nc
+    with ExitStack() as ctx:
+        keep = ctx.enter_context(tc.tile_pool(name="keep", bufs=1))
+        ring = ctx.enter_context(tc.tile_pool(name="ring", bufs=4))
+        stream = ctx.enter_context(tc.tile_pool(name="stream", bufs=1))
+        psum = ctx.enter_context(tc.psum_pool(name="psum", bufs=1))
+
+        def held(shape, dtype, name):
+            return keep.tile(shape, dtype, name=name, align_bytes=64)
+
+        def placed(shape, dtype, name, slot):
+            return stream.tile(shape, dtype, name=name, align_bytes=64, offset=slot * SLOT)
+
+        idx = keep.tile([P, S // 16], U16, name="idx")
+        idx2 = keep.tile([P, S2 // 16], U16, name="idx2")
+        tab_rows = held([P, T], U8, "tab_rows")
+        w4_rows = held([P, K], U8, "w4_rows")
+        planes = [held([P, PLANE], U8, f"planes{a}") for a in range(PASSES)]
+        b3_rows = held([P, P], F32, "b3_rows")
+        nc.gpsimd.memset(tab_rows[:, 0 : T // 2].bitcast(I32), 0)
+        nc.vector.memset(tab_rows[:, T // 2 : T].bitcast(I32), 0)
+        nc.vector.memset(w4_rows[:].bitcast(I32), 0)
+        warm = held([P, 16], F32, "warm")
+        nc.gpsimd.memset(warm[:, 0:8], 0.0)
+        nc.scalar.activation(warm[:, 8:9], warm[:, 0:1], ACT.Sigmoid)
+        nc.vector.memset(b3_rows[:], 0.0)
+        for a in range(PASSES):
+            nc.vector.memset(planes[a][:].bitcast(I32), 0)
+
+        def load_weight(w, a, col, width, name, slot):
+            raw = placed([P, PACK, width], F32, name, slot)
+            rows = w[a * KP : (a + 1) * KP, col : col + width]
+            nc.sync.dma_start(out=raw[:], in_=rows.rearrange("(p j) c -> p j c", j=PACK))
+            return raw
+
+        nc.sync.dma_start(idx[:], offs)
+        nc.sync.dma_start(idx2[:], offs2)
+        gain = held([P, PASSES, PACK], F32, "gain")
+        nc.sync.dma_start(out=gain[:], in_=gn.rearrange("(b p t) -> p b t", p=P, t=PACK))
+        w4_raw = []
+        for b in range(PASSES):
+            raw = held([P, PASSES, 2 * KP], U8, f"w4_raw{b}")
+            half = w4_words[:, :, 2 * b * KP : 2 * (b + 1) * KP]
+            nc.sync.dma_start(
+                out=raw[:].bitcast(I32), in_=half.rearrange("a p c -> p a c").bitcast(I32)
+            )
+            w4_raw.append(raw)
+        nc.sync.dma_start(
+            out=tab_rows[0:P:4, :].bitcast(I32),
+            in_=tab_scales.rearrange("a q t -> (a q) t").bitcast(I32),
+        )
+        nc.sync.dma_start(
+            out=w4_rows[0:P:4, :].bitcast(I32),
+            in_=w4_scales.rearrange("a q c -> (a q) c").bitcast(I32),
+        )
+        w1_raw = {}
+        w1_raw[0, 0] = load_weight(w1, 0, 0, KP, "w1_raw00", W1_SLOTS[0, 0])
+        tab = []
+        for a in range(PASSES):
+            words = placed([P, T], I32, f"tab{a}", 4 * a)
+            nc.sync.dma_start(
+                out=words[:], in_=tab_words[a].rearrange("p t i -> p (t i)").bitcast(I32)
+            )
+            tab.append(words)
+        w3_raw = {}
+
+        def load_w1(b, a):
+            w1_raw[b, a] = load_weight(w1, a, b * KP, KP, f"w1_raw{b}{a}", W1_SLOTS[b, a])
+
+        def load_w3(g, a):
+            col = sum(W3_WIDTHS[:g])
+            w3_raw[g, a] = load_weight(w3, a, col, W3_WIDTHS[g], f"w3_raw{g}{a}", W3_SLOTS[g, a])
+
+        nc.gpsimd.dma_start(out=b3_rows[0 : S2 // P, :], in_=b3.rearrange("(c p) -> c p", p=P))
+        ident = held([P, P], F32, "ident")
+        make_identity(nc, ident[:])
+        b3_turned = psum.tile([P, P], F32, name="b3_turned", tag="for_scalar", bufs=4)
+        nc.tensor.transpose(b3_turned[:], b3_rows[:], ident[:])
+        bias = held([P, S2 // P], F32, "bias")
+        nc.scalar.copy(bias[:], b3_turned[:, 0 : S2 // P])
+
+        picked = held([P, S + S2], U8, "picked")
+        nc.vector.tensor_copy(picked[:, V_COL:V2_COL], tab_rows[:].indirect(idx[:]))
+        nc.vector.tensor_copy(picked[:, V2_COL:W4_COL], tab_rows[:].indirect(idx2[:]))
+        staged = placed([P, PLANE], U8, "staged", 10)
+        nc.vector.tensor_copy(
+            staged[:, W4_COL:PLANE].rearrange("p (b t c i) -> p b c t i", b=PASSES, t=PACK, i=4),
+            w4_rows[:].rearrange("p (b c i t) -> p b c t i", b=PASSES, t=PACK, i=4),
+        )
+        nc.vector.tensor_copy(staged[:, V_COL:W4_COL].bitcast(I32), picked[:].bitcast(I32))
+        for a in range(PASSES):
+            for r in range(4):
+                first = 64 * a + 4 * r
+                queue = nc.scalar if r > 0 else nc.gpsimd
+                queue.dma_start(
+                    out=planes[a][r:P:32, :].bitcast(I32),
+                    in_=staged[first : 64 * (a + 1) : 16, :].bitcast(I32),
+                )
+
+        w4 = []
+        for b in range(PASSES):
+            dealt = placed([P, PASSES, 2 * KP], U8, f"w4_{b}", 12 + b)
+            nc.vector.tensor_copy(
+                dealt[:].bitcast(U16).rearrange("p a (t c i) -> p a c t i", t=PACK, i=4),
+                w4_raw[b][:]
+                .bitcast(U16)
+                .rearrange("p a (c i t) -> p a c t i", t=PACK, i=4),
+            )
+            w4.append(dealt)
+
+        def bf16_tile(width, slot):
+            if slot is None:
+                return ring.tile([P, PACK * width], BF16, name="grouped", align_bytes=64)
+            return placed([P, PACK * width], BF16, f"grouped{slot}", slot)
+
+        def copier(on_vector):
+            return nc.vector.tensor_copy if on_vector else nc.scalar.copy
+
+        def round_w1(b, a, on_vector, slot=None):
+            grouped = bf16_tile(KP, slot)
+            copier(on_vector)(
+                grouped[:].rearrange("p (t m j) -> p m j t", t=PACK, j=PACK),
+                w1_raw[b, a][:].rearrange("p j (m t) -> p m j t", t=PACK),
+            )
+            return grouped
+
+        def round_w3(g, a):
+            width = W3_WIDTHS[g]
+            grouped = bf16_tile(width, 13 if (g, a) == (0, 0) else None)
+            nc.scalar.copy(
+                grouped[:].rearrange("p (c i j) -> p c j i", i=4, j=PACK),
+                w3_raw[g, a][:].rearrange("p j (c i) -> p c j i", i=4),
+            )
+            return grouped
+
+        def quantize(grouped, width, name):
+            codes = held([P, width], U32, name + "_codes")
+            scales = held([P, width], U8, name + "_scales")
+            nc.vector.quantize_mx(out=codes[:].bitcast(FP8X4), scales=scales[:], in_=grouped[:])
+            return codes, scales
+
+        def gather(a, offsets, count, name):
+            words = held([P, count], U32, name)
+            nc.vector.tensor_copy(words[:], tab[a][:].bitcast(U32).indirect(offsets[:]))
+            return words
+
+        w1q = {}
+        w1q[0, 0] = quantize(round_w1(0, 0, False), KP, "w1q00")
+        load_w1(0, 1)
+        v = [gather(0, idx, S, "v0")]
+        v2 = [gather(0, idx2, S2, "v2_0")]
+        load_w1(1, 0)
+        load_w1(1, 1)
+        load_w3(0, 0)
+        v.append(gather(1, idx, S, "v1"))
+
+        def gained_own(b):
+            gown = held([P, PACK, S], F32, f"gown{b}")
+            for t in range(PACK):
+                bank = psum.tile([P, S], F32, name="own", tag="for_scalar", bufs=4)
+                c0 = b * KP + t * P
+                for a in range(PASSES):
+                    nc.tensor.matmul_mx(
+                        out=bank[:],
+                        lhsT=w4[b][:, a, 2 * t * P : 2 * (t + 1) * P].bitcast(FP4X4),
+                        lhsT_scale=planes[a][:, W4_COL + c0 : W4_COL + c0 + P],
+                        rhs=v[a][:].bitcast(FP8X4),
+                        rhs_scale=planes[a][:, V_COL:V2_COL],
+                        start=(a == 0),
+                        stop=(a == PASSES - 1),
+                    )
+                nc.scalar.activation(gown[:, t, :], bank[:], ACT.Copy, scale=gain[:, b, t : t + 1])
+            return gown
+
+        def asked_pass(b, a, bank, j0):
+            codes, scales = w1q[b, a]
+            for t in range(PACK):
+                nc.tensor.matmul_mx(
+                    out=bank[:, t, :],
+                    lhsT=codes[:, t * P : (t + 1) * P].bitcast(FP8X4),
+                    lhsT_scale=scales[:, t * P : (t + 1) * P],
+                    rhs=v[a][:, j0 : j0 + P].bitcast(FP8X4),
+                    rhs_scale=planes[a][:, V_COL + j0 : V_COL + j0 + P],
+                    start=(a == 0 and t == 0),
+                    stop=(a == PASSES - 1 and t == PACK - 1),
+                )
+
+        def open_asked(b):
+            banks = []
+            for j0 in range(0, S, P):
+                bank = psum.tile([P, PACK, P], F32, name="asked", tag="for_vector", bufs=4)
+                asked_pass(b, 0, bank, j0)
+                banks.append(bank)
+            return banks
+
+        def profile(b, banks, gown):
+            rounded = held([P, PACK * S], BF16, f"h{b}")
+            for bank, j0 in zip(banks, range(0, S, P)):
+                asked_pass(b, 1, bank, j0)
+                nc.vector.tensor_tensor(
+                    rounded[:, PACK * j0 : PACK * (j0 + P)].rearrange(
+                        "p (c i t) -> p c t i", i=4, t=PACK
+                    ),
+                    bank[:].rearrange("p t (c i) -> p c t i", i=4),
+                    gown[:, :, j0 : j0 + P].rearrange("p t (c i) -> p c t i", i=4),
+                    ALU.max,
+                )
+            return quantize(rounded, S, f"hq{b}")
+
+        gown0 = gained_own(0)
+        banks0 = open_asked(0)
+        v2.append(gather(1, idx2, S2, "v2_1"))
+        load_w3(0, 1)
+        load_w3(1, 0)
+        load_w3(1, 1)
+        w1q[0, 1] = quantize(round_w1(0, 1, True), KP, "w1q01")
+        load_w3(2, 0)
+        hq = [profile(0, banks0, gown0)]
+        w1q[1, 0] = quantize(round_w1(1, 0, False, 12), KP, "w1q10")
+        load_w3(2, 1)
+        gown1 = gained_own(1)
+        banks1 = open_asked(1)
+        w1q[1, 1] = quantize(round_w1(1, 1, True), KP, "w1q11")
+        hq.append(profile(1, banks1, gown1))
+
+        col = 0
+        for g, width in enumerate(W3_WIDTHS):
+            w3q = [quantize(round_w3(g, a), width, f"w3q{g}{a}") for a in range(PASSES)]
+            for m0 in range(0, width, P):
+                c = (col + m0) // P
+                lean = psum.tile([P, S], F32, name="lean", tag="for_scalar", bufs=4)
+                for a in range(PASSES):
+                    codes, scales = w3q[a]
+                    nc.tensor.matmul_mx(
+                        out=lean[:],
+                        lhsT=codes[:, m0 : m0 + P].bitcast(FP8X4),
+                        lhsT_scale=scales[:, m0 : m0 + P],
+                        rhs=v[a][:].bitcast(FP8X4),
+                        rhs_scale=planes[a][:, V_COL:V2_COL],
+                        start=(a == 0),
+                        stop=(a == PASSES - 1),
+                    )
+                gate = held([P, S], F32, f"gate{c}")
+                nc.scalar.activation(gate[:], lean[:], ACT.Sigmoid, bias=bias[:, c : c + 1])
+                match = psum.tile([P, S], F32, name="match", tag="for_vector", bufs=4)
+                for b in range(PASSES):
+                    codes, scales = hq[b]
+                    nc.tensor.matmul_mx(
+                        out=match[:],
+                        lhsT=v2[b][:, c * P : (c + 1) * P].bitcast(FP8X4),
+                        lhsT_scale=planes[b][:, V2_COL + c * P : V2_COL + (c + 1) * P],
+                        rhs=codes[:].bitcast(FP8X4),
+                        rhs_scale=scales[:],
+                        start=(b == 0),
+                        stop=(b == PASSES - 1),
+                    )
+                score = held([P, S], F32, f"score{c}")
+                nc.vector.tensor_tensor(score[:], match[:], gate[:], ALU.mult)
+                nc.sync.dma_start(out=out[c * P : (c + 1) * P, :], in_=score[:])
+            col = col + width

@@ -108,7 +108,7 @@ def tile_list_roommate_fit_scores_kernel(
         nc.gpsimd.dma_start(out=b3_rows[0 : S2 // P, :], in_=b3.rearrange("(c p) -> c p", p=P))
         ident = held([P, P], F32, "ident")
         make_identity(nc, ident[:])
-        b3_turned = psum.tile([P, P], F32, name="b3_turned", tag="for_scalar", bufs=4)
+        b3_turned = psum.tile([P, P], F32, name="b3_turned", tag="banks0", bufs=4)
         nc.tensor.transpose(b3_turned[:], b3_rows[:], ident[:])
         bias = held([P, S2 // P], F32, "bias")
         nc.scalar.copy(bias[:], b3_turned[:, 0 : S2 // P])
@@ -125,7 +125,7 @@ def tile_list_roommate_fit_scores_kernel(
         for a in range(PASSES):
             for r in range(4):
                 first = 64 * a + 4 * r
-                queue = nc.scalar if r > 0 else nc.gpsimd
+                queue = nc.gpsimd if a == 1 and r < 2 else nc.scalar
                 queue.dma_start(
                     out=planes[a][r:P:32, :].bitcast(I32),
                     in_=staged[first : 64 * (a + 1) : 16, :].bitcast(I32),
@@ -160,8 +160,8 @@ def tile_list_roommate_fit_scores_kernel(
 
         def round_w3(g, a):
             width = W3_WIDTHS[g]
-            grouped = bf16_tile(width, 13 if (g, a) == (0, 0) else None)
-            nc.scalar.copy(
+            grouped = bf16_tile(width, None)
+            copier(g == 2)(
                 grouped[:].rearrange("p (c i j) -> p c j i", i=4, j=PACK),
                 w3_raw[g, a][:].rearrange("p j (c i) -> p c j i", i=4),
             )
@@ -188,21 +188,30 @@ def tile_list_roommate_fit_scores_kernel(
         load_w3(0, 0)
         v.append(gather(1, idx, S, "v1"))
 
-        def gained_own(b):
-            gown = held([P, PACK, S], F32, f"gown{b}")
+        def own_pass(b, a, bank, t):
+            c0 = W4_COL + b * KP + t * P
+            nc.tensor.matmul_mx(
+                out=bank[:],
+                lhsT=w4[b][:, a, 2 * t * P : 2 * (t + 1) * P].bitcast(FP4X4),
+                lhsT_scale=planes[a][:, c0 : c0 + P],
+                rhs=v[a][:].bitcast(FP8X4),
+                rhs_scale=planes[a][:, V_COL:V2_COL],
+                start=(a == 0),
+                stop=(a == PASSES - 1),
+            )
+
+        def open_own(b):
+            banks = []
             for t in range(PACK):
-                bank = psum.tile([P, S], F32, name="own", tag="for_scalar", bufs=4)
-                c0 = b * KP + t * P
-                for a in range(PASSES):
-                    nc.tensor.matmul_mx(
-                        out=bank[:],
-                        lhsT=w4[b][:, a, 2 * t * P : 2 * (t + 1) * P].bitcast(FP4X4),
-                        lhsT_scale=planes[a][:, W4_COL + c0 : W4_COL + c0 + P],
-                        rhs=v[a][:].bitcast(FP8X4),
-                        rhs_scale=planes[a][:, V_COL:V2_COL],
-                        start=(a == 0),
-                        stop=(a == PASSES - 1),
-                    )
+                bank = psum.tile([P, S], F32, name="own", tag=f"banks{b}", bufs=4)
+                own_pass(b, 0, bank, t)
+                banks.append(bank)
+            return banks
+
+        def gained_own(b, banks):
+            gown = held([P, PACK, S], F32, f"gown{b}")
+            for t, bank in enumerate(banks):
+                own_pass(b, 1, bank, t)
                 nc.scalar.activation(gown[:, t, :], bank[:], ACT.Copy, scale=gain[:, b, t : t + 1])
             return gown
 
@@ -222,7 +231,7 @@ def tile_list_roommate_fit_scores_kernel(
         def open_asked(b):
             banks = []
             for j0 in range(0, S, P):
-                bank = psum.tile([P, PACK, P], F32, name="asked", tag="for_vector", bufs=4)
+                bank = psum.tile([P, PACK, P], F32, name="asked", tag=f"banks{b}", bufs=4)
                 asked_pass(b, 0, bank, j0)
                 banks.append(bank)
             return banks
@@ -239,32 +248,37 @@ def tile_list_roommate_fit_scores_kernel(
                     gown[:, :, j0 : j0 + P].rearrange("p t (c i) -> p c t i", i=4),
                     ALU.max,
                 )
-            return quantize(rounded, S, f"hq{b}")
+            return rounded
 
-        gown0 = gained_own(0)
-        banks0 = open_asked(0)
+        own = [open_own(b) for b in range(PASSES)]
+        gown = [gained_own(b, own[b]) for b in range(PASSES)]
+        asked0 = open_asked(0)
         v2.append(gather(1, idx2, S2, "v2_1"))
         load_w3(0, 1)
         load_w3(1, 0)
         load_w3(1, 1)
         w1q[0, 1] = quantize(round_w1(0, 1, True), KP, "w1q01")
         load_w3(2, 0)
-        hq = [profile(0, banks0, gown0)]
-        w1q[1, 0] = quantize(round_w1(1, 0, False, 12), KP, "w1q10")
+        w1q[1, 0] = quantize(round_w1(1, 0, True), KP, "w1q10")
         load_w3(2, 1)
-        gown1 = gained_own(1)
-        banks1 = open_asked(1)
-        w1q[1, 1] = quantize(round_w1(1, 1, True), KP, "w1q11")
-        hq.append(profile(1, banks1, gown1))
+        h0 = profile(0, asked0, gown[0])
+        asked1 = open_asked(1)
+        w1q[1, 1] = quantize(round_w1(1, 1, False), KP, "w1q11")
+        hq = [quantize(h0, S, "hq0")]
+        w3q = {}
+        w3q[0, 0] = quantize(round_w3(0, 0), W3_WIDTHS[0], "w3q00")
+        hq.append(quantize(profile(1, asked1, gown[1]), S, "hq1"))
+        for g, a in ((0, 1), (1, 0), (1, 1), (2, 0), (2, 1)):
+            w3q[g, a] = quantize(round_w3(g, a), W3_WIDTHS[g], f"w3q{g}{a}")
 
+        gates = [placed([P, 4, S], F32, "gates0", 6), held([P, 4, S], F32, "gates1")]
         col = 0
         for g, width in enumerate(W3_WIDTHS):
-            w3q = [quantize(round_w3(g, a), width, f"w3q{g}{a}") for a in range(PASSES)]
             for m0 in range(0, width, P):
                 c = (col + m0) // P
-                lean = psum.tile([P, S], F32, name="lean", tag="for_scalar", bufs=4)
+                lean = psum.tile([P, S], F32, name="lean", tag="banks0", bufs=4)
                 for a in range(PASSES):
-                    codes, scales = w3q[a]
+                    codes, scales = w3q[g, a]
                     nc.tensor.matmul_mx(
                         out=lean[:],
                         lhsT=codes[:, m0 : m0 + P].bitcast(FP8X4),
@@ -274,9 +288,9 @@ def tile_list_roommate_fit_scores_kernel(
                         start=(a == 0),
                         stop=(a == PASSES - 1),
                     )
-                gate = held([P, S], F32, f"gate{c}")
-                nc.scalar.activation(gate[:], lean[:], ACT.Sigmoid, bias=bias[:, c : c + 1])
-                match = psum.tile([P, S], F32, name="match", tag="for_vector", bufs=4)
+                gate = gates[c // 4][:, c % 4, :]
+                nc.scalar.activation(gate, lean[:], ACT.Sigmoid, bias=bias[:, c : c + 1])
+                match = psum.tile([P, S], F32, name="match", tag="banks1", bufs=4)
                 for b in range(PASSES):
                     codes, scales = hq[b]
                     nc.tensor.matmul_mx(
@@ -289,6 +303,6 @@ def tile_list_roommate_fit_scores_kernel(
                         stop=(b == PASSES - 1),
                     )
                 score = held([P, S], F32, f"score{c}")
-                nc.vector.tensor_tensor(score[:], match[:], gate[:], ALU.mult)
+                nc.vector.tensor_tensor(score[:], match[:], gate, ALU.mult)
                 nc.sync.dma_start(out=out[c * P : (c + 1) * P, :], in_=score[:])
             col = col + width

from contextlib import ExitStack

import concourse.mybir as mybir
from concourse.masks import make_identity

K, T, S, S2 = 1024, 4096, 512, 1024
FLOPS = 2 * K * S * (K + K + S2 + S2)

F32 = mybir.dt.float32
BF16 = mybir.dt.bfloat16
I32 = mybir.dt.int32
U32 = mybir.dt.uint32
U16 = mybir.dt.uint16
U8 = mybir.dt.uint8
FP8X4 = mybir.dt.float8_e4m3fn_x4
FP4X4 = mybir.dt.float4_e2m1fn_x4
ACT = mybir.ActivationFunctionType
ALU = mybir.AluOpType

P = 128
PACK = 4
KP = P * PACK
PASSES = K // KP
W3_WIDTHS = (512, 256, 256)
SLOT = 4096
W1_SLOTS = {(0, 0): 8, (0, 1): 8, (1, 0): 0, (1, 1): 2}
W3_SLOTS = {(0, 0): 10, (0, 1): 4, (1, 0): 6, (1, 1): 7, (2, 0): 8, (2, 1): 0}
V_COL, V2_COL, W4_COL = 0, S, S + S2
PLANE = S + S2 + K


def tile_list_roommate_fit_scores_kernel(
    tc, tab_words, tab_scales, offs, offs2, w1, w4_words, w4_scales, gn, w3, b3, out
):
    nc = tc.nc
    with ExitStack() as ctx:
        keep = ctx.enter_context(tc.tile_pool(name="keep", bufs=1))
        ring = ctx.enter_context(tc.tile_pool(name="ring", bufs=4))
        stream = ctx.enter_context(tc.tile_pool(name="stream", bufs=1))
        psum = ctx.enter_context(tc.psum_pool(name="psum", bufs=1))

        def held(shape, dtype, name):
            return keep.tile(shape, dtype, name=name, align_bytes=64)

        def placed(shape, dtype, name, slot):
            return stream.tile(shape, dtype, name=name, align_bytes=64, offset=slot * SLOT)

        idx = keep.tile([P, S // 16], U16, name="idx")
        idx2 = keep.tile([P, S2 // 16], U16, name="idx2")
        tab_rows = held([P, T], U8, "tab_rows")
        w4_rows = held([P, K], U8, "w4_rows")
        planes = [held([P, PLANE], U8, f"planes{a}") for a in range(PASSES)]
        b3_rows = held([P, P], F32, "b3_rows")
        nc.gpsimd.memset(tab_rows[:, 0 : T // 2].bitcast(I32), 0)
        nc.vector.memset(tab_rows[:, T // 2 : T].bitcast(I32), 0)
        nc.vector.memset(w4_rows[:].bitcast(I32), 0)
        warm = held([P, 16], F32, "warm")
        nc.gpsimd.memset(warm[:, 0:8], 0.0)
        nc.scalar.activation(warm[:, 8:9], warm[:, 0:1], ACT.Sigmoid)
        nc.vector.memset(b3_rows[:], 0.0)
        for a in range(PASSES):
            nc.vector.memset(planes[a][:].bitcast(I32), 0)

        def load_weight(w, a, col, width, name, slot):
            raw = placed([P, PACK, width], F32, name, slot)
            rows = w[a * KP : (a + 1) * KP, col : col + width]
            nc.sync.dma_start(out=raw[:], in_=rows.rearrange("(p j) c -> p j c", j=PACK))
            return raw

        nc.sync.dma_start(idx[:], offs)
        nc.sync.dma_start(idx2[:], offs2)
        gain = held([P, PASSES, PACK], F32, "gain")
        nc.sync.dma_start(out=gain[:], in_=gn.rearrange("(b p t) -> p b t", p=P, t=PACK))
        w4_raw = []
        for b in range(PASSES):
            raw = held([P, PASSES, 2 * KP], U8, f"w4_raw{b}")
            half = w4_words[:, :, 2 * b * KP : 2 * (b + 1) * KP]
            nc.sync.dma_start(
                out=raw[:].bitcast(I32), in_=half.rearrange("a p c -> p a c").bitcast(I32)
            )
            w4_raw.append(raw)
        nc.sync.dma_start(
            out=tab_rows[0:P:4, :].bitcast(I32),
            in_=tab_scales.rearrange("a q t -> (a q) t").bitcast(I32),
        )
        nc.sync.dma_start(
            out=w4_rows[0:P:4, :].bitcast(I32),
            in_=w4_scales.rearrange("a q c -> (a q) c").bitcast(I32),
        )
        w1_raw = {}
        w1_raw[0, 0] = load_weight(w1, 0, 0, KP, "w1_raw00", W1_SLOTS[0, 0])
        tab = []
        for a in range(PASSES):
            words = placed([P, T], I32, f"tab{a}", 4 * a)
            nc.sync.dma_start(
                out=words[:], in_=tab_words[a].rearrange("p t i -> p (t i)").bitcast(I32)
            )
            tab.append(words)
        w3_raw = {}

        def load_w1(b, a):
            w1_raw[b, a] = load_weight(w1, a, b * KP, KP, f"w1_raw{b}{a}", W1_SLOTS[b, a])

        def load_w3(g, a):
            col = sum(W3_WIDTHS[:g])
            w3_raw[g, a] = load_weight(w3, a, col, W3_WIDTHS[g], f"w3_raw{g}{a}", W3_SLOTS[g, a])

        nc.gpsimd.dma_start(out=b3_rows[0 : S2 // P, :], in_=b3.rearrange("(c p) -> c p", p=P))
        ident = held([P, P], F32, "ident")
        make_identity(nc, ident[:])
        b3_turned = psum.tile([P, P], F32, name="b3_turned", tag="banks0", bufs=4)
        nc.tensor.transpose(b3_turned[:], b3_rows[:], ident[:])
        bias = held([P, S2 // P], F32, "bias")
        nc.scalar.copy(bias[:], b3_turned[:, 0 : S2 // P])

        picked = held([P, S + S2], U8, "picked")
        nc.vector.tensor_copy(picked[:, V_COL:V2_COL], tab_rows[:].indirect(idx[:]))
        nc.vector.tensor_copy(picked[:, V2_COL:W4_COL], tab_rows[:].indirect(idx2[:]))
        staged = placed([P, PLANE], U8, "staged", 10)
        nc.vector.tensor_copy(
            staged[:, W4_COL:PLANE].rearrange("p (b t c i) -> p b c t i", b=PASSES, t=PACK, i=4),
            w4_rows[:].rearrange("p (b c i t) -> p b c t i", b=PASSES, t=PACK, i=4),
        )
        nc.vector.tensor_copy(staged[:, V_COL:W4_COL].bitcast(I32), picked[:].bitcast(I32))
        for a in range(PASSES):
            for r in range(4):
                first = 64 * a + 4 * r
                queue = nc.gpsimd if a == 1 and r < 2 else nc.scalar
                queue.dma_start(
                    out=planes[a][r:P:32, :].bitcast(I32),
                    in_=staged[first : 64 * (a + 1) : 16, :].bitcast(I32),
                )

        w4 = []
        for b in range(PASSES):
            dealt = placed([P, PASSES, 2 * KP], U8, f"w4_{b}", 12 + b)
            nc.vector.tensor_copy(
                dealt[:].bitcast(U16).rearrange("p a (t c i) -> p a c t i", t=PACK, i=4),
                w4_raw[b][:]
                .bitcast(U16)
                .rearrange("p a (c i t) -> p a c t i", t=PACK, i=4),
            )
            w4.append(dealt)

        def bf16_tile(width, slot):
            if slot is None:
                return ring.tile([P, PACK * width], BF16, name="grouped", align_bytes=64)
            return placed([P, PACK * width], BF16, f"grouped{slot}", slot)

        def copier(on_vector):
            return nc.vector.tensor_copy if on_vector else nc.scalar.copy

        def round_w1(b, a, on_vector, slot=None):
            grouped = bf16_tile(KP, slot)
            copier(on_vector)(
                grouped[:].rearrange("p (t m j) -> p m j t", t=PACK, j=PACK),
                w1_raw[b, a][:].rearrange("p j (m t) -> p m j t", t=PACK),
            )
            return grouped

        def round_w3(g, a):
            width = W3_WIDTHS[g]
            grouped = bf16_tile(width, None)
            copier(g == 2)(
                grouped[:].rearrange("p (c i j) -> p c j i", i=4, j=PACK),
                w3_raw[g, a][:].rearrange("p j (c i) -> p c j i", i=4),
            )
            return grouped

        def quantize(grouped, width, name):
            codes = held([P, width], U32, name + "_codes")
            scales = held([P, width], U8, name + "_scales")
            nc.vector.quantize_mx(out=codes[:].bitcast(FP8X4), scales=scales[:], in_=grouped[:])
            return codes, scales

        def gather(a, offsets, count, name):
            words = held([P, count], U32, name)
            nc.vector.tensor_copy(words[:], tab[a][:].bitcast(U32).indirect(offsets[:]))
            return words

        w1q = {}
        w1q[0, 0] = quantize(round_w1(0, 0, False), KP, "w1q00")
        load_w1(0, 1)
        v = [gather(0, idx, S, "v0")]
        v2 = [gather(0, idx2, S2, "v2_0")]
        load_w1(1, 0)
        load_w1(1, 1)
        load_w3(0, 0)
        v.append(gather(1, idx, S, "v1"))

        def own_pass(b, a, bank, t):
            c0 = W4_COL + b * KP + t * P
            nc.tensor.matmul_mx(
                out=bank[:],
                lhsT=w4[b][:, a, 2 * t * P : 2 * (t + 1) * P].bitcast(FP4X4),
                lhsT_scale=planes[a][:, c0 : c0 + P],
                rhs=v[a][:].bitcast(FP8X4),
                rhs_scale=planes[a][:, V_COL:V2_COL],
                start=(a == 0),
                stop=(a == PASSES - 1),
            )

        def open_own(b):
            banks = []
            for t in range(PACK):
                bank = psum.tile([P, S], F32, name="own", tag=f"banks{b}", bufs=4)
                own_pass(b, 0, bank, t)
                banks.append(bank)
            return banks

        def gained_own(b, banks):
            gown = held([P, PACK, S], F32, f"gown{b}")
            for t, bank in enumerate(banks):
                own_pass(b, 1, bank, t)
                nc.scalar.activation(gown[:, t, :], bank[:], ACT.Copy, scale=gain[:, b, t : t + 1])
            return gown

        def asked_pass(b, a, bank, j0):
            codes, scales = w1q[b, a]
            for t in range(PACK):
                nc.tensor.matmul_mx(
                    out=bank[:, t, :],
                    lhsT=codes[:, t * P : (t + 1) * P].bitcast(FP8X4),
                    lhsT_scale=scales[:, t * P : (t + 1) * P],
                    rhs=v[a][:, j0 : j0 + P].bitcast(FP8X4),
                    rhs_scale=planes[a][:, V_COL + j0 : V_COL + j0 + P],
                    start=(a == 0 and t == 0),
                    stop=(a == PASSES - 1 and t == PACK - 1),
                )

        def open_asked(b):
            banks = []
            for j0 in range(0, S, P):
                bank = psum.tile([P, PACK, P], F32, name="asked", tag=f"banks{b}", bufs=4)
                asked_pass(b, 0, bank, j0)
                banks.append(bank)
            return banks

        def profile(b, banks, gown):
            rounded = held([P, PACK * S], BF16, f"h{b}")
            for bank, j0 in zip(banks, range(0, S, P)):
                asked_pass(b, 1, bank, j0)
                nc.vector.tensor_tensor(
                    rounded[:, PACK * j0 : PACK * (j0 + P)].rearrange(
                        "p (c i t) -> p c t i", i=4, t=PACK
                    ),
                    bank[:].rearrange("p t (c i) -> p c t i", i=4),
                    gown[:, :, j0 : j0 + P].rearrange("p t (c i) -> p c t i", i=4),
                    ALU.max,
                )
            return rounded

        own = [open_own(b) for b in range(PASSES)]
        gown = [gained_own(b, own[b]) for b in range(PASSES)]
        asked0 = open_asked(0)
        v2.append(gather(1, idx2, S2, "v2_1"))
        load_w3(0, 1)
        load_w3(1, 0)
        load_w3(1, 1)
        w1q[0, 1] = quantize(round_w1(0, 1, True), KP, "w1q01")
        load_w3(2, 0)
        w1q[1, 0] = quantize(round_w1(1, 0, True), KP, "w1q10")
        load_w3(2, 1)
        h0 = profile(0, asked0, gown[0])
        asked1 = open_asked(1)
        w1q[1, 1] = quantize(round_w1(1, 1, False), KP, "w1q11")
        hq = [quantize(h0, S, "hq0")]
        w3q = {}
        w3q[0, 0] = quantize(round_w3(0, 0), W3_WIDTHS[0], "w3q00")
        hq.append(quantize(profile(1, asked1, gown[1]), S, "hq1"))
        for g, a in ((0, 1), (1, 0), (1, 1), (2, 0), (2, 1)):
            w3q[g, a] = quantize(round_w3(g, a), W3_WIDTHS[g], f"w3q{g}{a}")

        gates = [placed([P, 4, S], F32, "gates0", 6), held([P, 4, S], F32, "gates1")]
        col = 0
        for g, width in enumerate(W3_WIDTHS):
            for m0 in range(0, width, P):
                c = (col + m0) // P
                lean = psum.tile([P, S], F32, name="lean", tag="banks0", bufs=4)
                for a in range(PASSES):
                    codes, scales = w3q[g, a]
                    nc.tensor.matmul_mx(
                        out=lean[:],
                        lhsT=codes[:, m0 : m0 + P].bitcast(FP8X4),
                        lhsT_scale=scales[:, m0 : m0 + P],
                        rhs=v[a][:].bitcast(FP8X4),
                        rhs_scale=planes[a][:, V_COL:V2_COL],
                        start=(a == 0),
                        stop=(a == PASSES - 1),
                    )
                gate = gates[c // 4][:, c % 4, :]
                nc.scalar.activation(gate, lean[:], ACT.Sigmoid, bias=bias[:, c : c + 1])
                match = psum.tile([P, S], F32, name="match", tag="banks1", bufs=4)
                for b in range(PASSES):
                    codes, scales = hq[b]
                    nc.tensor.matmul_mx(
                        out=match[:],
                        lhsT=v2[b][:, c * P : (c + 1) * P].bitcast(FP8X4),
                        lhsT_scale=planes[b][:, V2_COL + c * P : V2_COL + (c + 1) * P],
                        rhs=codes[:].bitcast(FP8X4),
                        rhs_scale=scales[:],
                        start=(b == 0),
                        stop=(b == PASSES - 1),
                    )
                score = held([P, S], F32, f"score{c}")
                nc.vector.tensor_tensor(score[:], match[:], gate, ALU.mult)
                nc.sync.dma_start(out=out[c * P : (c + 1) * P, :], in_=score[:])
            col = col + width
